import numpy as np
import ml_dtypes


def mxq(x, axis, fmt="e4m3"):
    dtype, down = {"e4m3": (ml_dtypes.float8_e4m3fn, 7), "e5m2": (ml_dtypes.float8_e5m2, 14)}[fmt]
    v = np.moveaxis(np.asarray(x, np.float32).astype(ml_dtypes.bfloat16).astype(np.float64), axis, -1)
    blocks = v.reshape(v.shape[:-1] + (-1, 32))
    amax = np.abs(blocks).max(-1, keepdims=True)
    byte = np.maximum(np.where(amax > 0, np.frexp(amax)[1] - 1 + 127, 0) - down, 1)
    scale = np.exp2(byte - 127.0)
    codes = (blocks / scale).astype(np.float32).astype(dtype).astype(np.float64)
    return np.moveaxis((codes * scale).reshape(v.shape), -1, axis)


WIDE = False


def mx_kscale(k):
    if not WIDE:
        return np.ones(k)
    levels = np.array([24, -24, 12, -12, 0])
    if k % 512:
        return np.exp2(np.random.permutation(np.resize(levels, k // 32))).repeat(32)
    a = np.empty((k // 512, 16))
    for p in range(k // 512):
        a[p, :8] = np.random.permutation(np.resize(levels, 8))
        for g in range(8):
            far = levels[np.abs(levels - a[p, g]) >= 10]
            a[p, g + 8] = far[np.random.randint(len(far))]
    return np.exp2(a.ravel()).repeat(32)


def f64(x):
    return np.asarray(x).astype(np.float64)


def striped8(idx):
    return np.concatenate([v.reshape(-1, 16).T for v in idx]).astype(np.uint16)


def unstriped8(offs):
    return np.stack([offs[16 * g:16 * g + 16].T.reshape(-1) for g in range(8)]).astype(np.int64)


E2M1 = np.array([0.0, 0.5, 1.0, 1.5, 2.0, 3.0, 4.0, 6.0, -0.0, -0.5, -1.0, -1.5, -2.0, -3.0, -4.0, -6.0])


def pack_weight(w, fmt):
    k, n = w.shape
    w = f64(np.asarray(w, np.float32).astype(ml_dtypes.bfloat16)).reshape(k // 32, 32, n)
    amax = np.abs(w).max(1)
    if fmt == "e4m3":
        byte = np.frexp(amax)[1] - 1 + 127 - 7
    else:
        mant, ex = np.frexp(amax / 6.0)
        byte = np.where(mant > 0.5, ex, ex - 1) + 127
    byte = np.clip(np.where(amax > 0, byte, 1), 1, 254)
    scaled = (w * np.exp2(127.0 - byte)[:, None, :]).reshape(k, n).astype(np.float32)
    by_word = np.ascontiguousarray(scaled.reshape(k // 512, 128, 4, n).transpose(0, 1, 3, 2))
    if fmt == "e4m3":
        words = by_word.astype(ml_dtypes.float8_e4m3fn).view(np.uint8)
    else:
        c = by_word.astype(ml_dtypes.float4_e2m1fn).view(np.uint8) & 0xF
        words = (c[..., 0::2] | (c[..., 1::2] << 4)).reshape(k // 512, 128, 2 * n)
    return np.ascontiguousarray(words), np.ascontiguousarray(byte.astype(np.uint8).reshape(k // 512, 16, n))


def unpack_weight(words, scales, fmt):
    g, _, n = scales.shape
    words = np.ascontiguousarray(words).reshape(g, 128, n, -1)
    if fmt == "e4m3":
        vals = words.view(ml_dtypes.float8_e4m3fn).astype(np.float64)
    else:
        nib = np.empty((g, 128, n, 4), np.uint8)
        nib[..., 0::2] = words & 0xF
        nib[..., 1::2] = words >> 4
        vals = E2M1[nib]
    vals = vals * np.repeat(np.exp2(scales.astype(np.float64) - 127.0), 8, axis=1)[..., None]
    return vals.transpose(0, 1, 3, 2).reshape(g * 512, n)


def planes(y):
    n, m = y.shape
    v = y.astype(np.float32).astype(ml_dtypes.bfloat16).astype(np.float64).reshape(n // 32, 32, m)
    top = np.abs(v).max(1)
    byte = np.clip(np.where(top > 0, np.frexp(top)[1] - 1 + 127 - 7, 1), 1, 254)
    codes = (v * np.exp2(127.0 - byte)[:, None, :]).reshape(n, m).astype(np.float32).astype(ml_dtypes.float8_e4m3fn).view(np.uint8)
    words = codes.reshape(n // 512, 128, 4, m).transpose(0, 1, 3, 2)
    return np.ascontiguousarray(words), np.ascontiguousarray(byte.astype(np.uint8).reshape(n // 512, 16, m))


def gelu(f):
    return 0.5 * f * (1.0 + np.tanh(np.sqrt(2.0 / np.pi) * (f + 0.044715 * f**3)))


K, R, N, T, J = 1024, 1024, 512, 2048, 1024


def setup_inputs():
    n = np.random.standard_normal
    s = mx_kscale(K)[:, None]
    u = mx_kscale(R)[:, None]
    p_wd = pack_weight(n((R, N)) / np.sqrt(R) / u, "e2m1")
    return {
        "xT": (n((K, T)) * s).astype(np.float32),
        "wgt": np.repeat(np.random.uniform(0.5, 2.0, (8, J)), 16, axis=0).astype(np.float32),
        "wg": (n((K, R)) / np.sqrt(K) / s).astype(np.float32),
        "wu": (n((K, R)) / np.sqrt(K) / s * u.T).astype(np.float32),
        "wd_words": p_wd[0],
        "wd_scales": p_wd[1],
        "g": (n((N, J))).astype(np.float32),
        "offs": striped8(np.stack([np.random.permutation(T)[:J] for _ in range(8)])),
    }


def reference(xT, wgt, wg, wu, wd_words, wd_scales, g, offs):
    idx = unstriped8(offs)
    rows = np.arange(K)
    xg = f64(wgt)[rows // 4 % 128] * f64(xT)[rows[:, None], idx[rows % 512 // 64]]
    xT_ = mxq(xg, 0, "e4m3")
    wg_ = mxq(f64(wg), 0, "e4m3")
    wu_ = mxq(f64(wu), 0, "e4m3")
    ga = wg_.T @ xT_
    ub = wu_.T @ xT_
    h = gelu(ga) * ub
    h_ = mxq(h, 0, "e4m3")
    wd_ = unpack_weight(wd_words, wd_scales, "e2m1")
    y = wd_.T @ h_
    out_0 = y * f64(g)
    return (out_0,) + planes(out_0)

@@ -1,0 +1,272 @@
+from contextlib import ExitStack
+
+import concourse.mybir as mybir
+
+K, R, N, T, J = 1024, 1024, 512, 2048, 1024
+FLOPS = 2 * K * R * J * 2 + 2 * R * N * J
+
+F32 = mybir.dt.float32
+BF16 = mybir.dt.bfloat16
+I32 = mybir.dt.int32
+U32 = mybir.dt.uint32
+U16 = mybir.dt.uint16
+U8 = mybir.dt.uint8
+FP8X4 = mybir.dt.float8_e4m3fn_x4
+FP4X4 = mybir.dt.float4_e2m1fn_x4
+MULT = mybir.AluOpType.mult
+GELU = mybir.ActivationFunctionType.Gelu_apprx_tanh
+
+P = 128
+PACK = 4
+PASS = P * PACK
+JQ = 256
+NQ = J // JQ
+RAW_BUFS = 9
+TAIL = [("scalar", 0, 128), ("vector", 128, 256)]
+
+
+def tile_list_gelu_mulP_kernel(tc, xT, wgt, wg, wu, wd_words, wd_scales, g, offs, out_0, out_1, out_2):
+    nc = tc.nc
+
+    with ExitStack() as ctx:
+        keep = ctx.enter_context(tc.tile_pool(name="keep", bufs=1))
+        raw = ctx.enter_context(tc.tile_pool(name="raw", bufs=RAW_BUFS))
+        stage = ctx.enter_context(tc.tile_pool(name="stage", bufs=2))
+        psum = ctx.enter_context(tc.psum_pool(name="psum", bufs=1))
+
+        def copy_on(engine, out, in_):
+            if engine == "vector":
+                nc.vector.tensor_copy(out=out, in_=in_)
+            else:
+                nc.scalar.copy(out=out, in_=in_)
+
+        def quantize(rounded, width, name):
+            codes = keep.tile([P, width], U32, name=name + "_codes", align_bytes=64)
+            scales = keep.tile([P, width], U8, name=name + "_scales", align_bytes=64)
+            nc.vector.quantize_mx(out=codes[:].bitcast(FP8X4), scales=scales[:], in_=rounded)
+            return codes, scales
+
+        offsets = keep.tile([P, J // 16], U16, name="offsets")
+        wd_raw = keep.tile([P, 2, 2 * N], U8, name="wd_raw")
+        wds_raw = keep.tile([P, 2, N], U8, name="wds_raw")
+        place_w = keep.tile([P, J], F32, name="place_w")
+        x_planes = {}
+        w_raw = {}
+        gate = {}
+
+        def load_wd():
+            nc.sync.dma_start(out=wd_raw[:].bitcast(I32), in_=wd_words.rearrange("a p n -> p a n").bitcast(I32))
+
+        def load_wds():
+            for q in range(4):
+                nc.sync.dma_start(
+                    out=wds_raw[32 * q : 32 * q + 4, :, :].bitcast(I32),
+                    in_=wd_scales[:, 4 * q : 4 * q + 4, :].rearrange("a r n -> r a n").bitcast(I32),
+                )
+
+        def load_place(c0, c1):
+            nc.sync.dma_start(out=place_w[:, c0:c1], in_=wgt[:, c0:c1])
+
+        def load_x(a, i):
+            rows = xT[a * PASS : (a + 1) * PASS, :].rearrange("(p i) t -> p i t", i=PACK)
+            x_planes[a, i] = raw.tile([P, T], F32, name="x_plane", tag="raw")
+            nc.sync.dma_start(out=x_planes[a, i][:], in_=rows[:, i, :])
+
+        def load_w(wname, a, b):
+            w = {"wg": wg, "wu": wu}[wname]
+            w_raw[wname, a, b] = raw.tile([P, PACK, PASS], F32, name="w_raw", tag="raw")
+            block = w[a * PASS : (a + 1) * PASS, b * PASS : (b + 1) * PASS]
+            nc.sync.dma_start(out=w_raw[wname, a, b][:], in_=block.rearrange("(p i) c -> p i c", i=PACK))
+
+        def load_g(h):
+            gate[h] = raw.tile([P, PACK, 512], F32, name="gate", tag="raw")
+            nc.sync.dma_start(out=gate[h][:], in_=g[:, h * 512 : (h + 1) * 512].rearrange("(p t) j -> p t j", t=PACK))
+
+        nc.vector.memset(wds_raw[:].bitcast(I32), 0)
+        nc.sync.dma_start(offsets[:], offs)
+        load_wd()
+        load_wds()
+        load_place(0, 1024)
+        load_x(0, 0)
+        load_x(0, 1)
+        load_x(0, 2)
+        load_x(0, 3)
+        load_x(1, 0)
+        load_x(1, 1)
+        load_x(1, 2)
+        load_w("wg", 0, 0)
+        load_x(1, 3)
+        load_w("wg", 1, 0)
+        load_w("wu", 0, 0)
+        load_w("wu", 1, 0)
+        load_w("wg", 0, 1)
+        load_w("wg", 1, 1)
+        load_w("wu", 0, 1)
+        load_w("wu", 1, 1)
+        load_g(0)
+        load_g(1)
+
+        warm = keep.tile([P, 1], F32, name="warm")
+        nc.scalar.activation(out=warm[:], in_=place_w[:, 0:1], func=GELU)
+
+        wd_codes = keep.tile([P, 2, 2 * N], U8, name="wd_codes", align_bytes=64)
+        wd_planes = keep.tile([P, 2, N], U8, name="wd_planes", align_bytes=64)
+        nc.vector.tensor_copy(
+            out=wd_codes[:].bitcast(U16).rearrange("p a (t m) -> p a m t", t=PACK),
+            in_=wd_raw[:].bitcast(U16).rearrange("p a (m t) -> p a m t", t=PACK),
+        )
+        nc.vector.tensor_copy(
+            out=wd_planes[:].rearrange("p a (t m) -> p a t m", t=PACK),
+            in_=wds_raw[:].rearrange("p a (m t) -> p a t m", t=PACK),
+        )
+
+        xq = {}
+
+        def gather_pass(a):
+            picked = stage.tile([P, PACK, J], F32, name="picked")
+            for i in range(PACK):
+                nc.vector.tensor_tensor(picked[:, i, :], x_planes[a, i][:].indirect(offsets[:]), place_w[:], MULT)
+            return picked
+
+        def quantize_x(a, picked, engines):
+            for jq in range(NQ):
+                rounded = stage.tile([P, JQ, PACK], BF16, name="x_rounded", bufs=4, align_bytes=64)
+                copy_on(
+                    engines[jq],
+                    rounded[:].rearrange("p (c e) i -> p c i e", e=4),
+                    picked[:, :, jq * JQ : (jq + 1) * JQ].rearrange("p i (c e) -> p c i e", e=4),
+                )
+                xq[a, jq] = quantize(rounded[:].rearrange("p j i -> p (j i)"), JQ, "x%d%d" % (a, jq))
+
+        wq = {}
+
+        def quantize_w(wname, a, b, engine):
+            rounded = stage.tile([P, PACK * PASS], BF16, name="w_rounded", bufs=3, align_bytes=64)
+            copy_on(
+                engine,
+                rounded[:].rearrange("p (t m i) -> p m i t", t=PACK, i=PACK),
+                w_raw[wname, a, b][:].rearrange("p i (m t) -> p m i t", t=PACK),
+            )
+            wq[wname, a, b] = quantize(rounded[:], PASS, "%s%d%d" % (wname, a, b))
+
+        def first_product(out, wname, b, t, jq, cols):
+            for a in range(2):
+                w_codes, w_scales = wq[wname, a, b]
+                x_codes, x_scales = xq[a, jq]
+                nc.tensor.matmul_mx(
+                    out=out,
+                    lhsT=w_codes[:, t * P : (t + 1) * P].bitcast(FP8X4),
+                    lhsT_scale=w_scales[:, t * P : (t + 1) * P],
+                    rhs=x_codes[:, cols].bitcast(FP8X4),
+                    rhs_scale=x_scales[:, cols],
+                    start=(a == 0),
+                    stop=(a == 1),
+                )
+
+        act = {}
+
+        def gate_branch(b, jq):
+            act[b, jq] = keep.tile([P, 2, JQ, 2], F32, name="act%d%d" % (b, jq))
+            for tp in range(2):
+                bank = psum.tile([P, 2, JQ], F32, name="ga_bank", bufs=3)
+                for e in range(2):
+                    first_product(bank[:, e, :], "wg", b, 2 * tp + e, jq, slice(0, JQ))
+                nc.scalar.activation(out=act[b, jq][:, tp, :, :], in_=bank[:].rearrange("p e j -> p j e"), func=GELU)
+
+        hq = {}
+
+        def up_branch(b, jq):
+            rounded = stage.tile([P, JQ, PACK], BF16, name="h_rounded", bufs=3, align_bytes=64)
+            for half in range(2):
+                cols = slice(half * P, (half + 1) * P)
+                bank = psum.tile([P, PACK, P], F32, name="ub_bank", bufs=3)
+                for t in range(PACK):
+                    first_product(bank[:, t, :], "wu", b, t, jq, cols)
+                nc.vector.tensor_tensor(
+                    rounded[:, cols, :].rearrange("p j (tp e) -> p j tp e", e=2),
+                    bank[:].rearrange("p (tp e) j -> p j tp e", e=2),
+                    act[b, jq][:, :, cols, :].rearrange("p tp j e -> p j tp e"),
+                    MULT,
+                )
+            hq[b, jq] = quantize(rounded[:].rearrange("p j t -> p (j t)"), JQ, "h%d%d" % (b, jq))
+
+        out_codes = keep.tile([P, J], U32, name="out_codes", align_bytes=64)
+        out_scales = keep.tile([P, J], U8, name="out_scales", align_bytes=64)
+        out_rows = out_0.rearrange("(p t) j -> p t j", t=PACK)
+        out_words = out_1[0].rearrange("p j t -> p (j t)").bitcast(I32)
+
+        def down(jq):
+            result = raw.tile([P, PACK, JQ], F32, name="result", tag="raw")
+            jcols = slice(jq * JQ, (jq + 1) * JQ)
+            for half in range(2):
+                cols = slice(half * P, (half + 1) * P)
+                bank = psum.tile([P, PACK, P], F32, name="y_bank", bufs=2)
+                for t in range(PACK):
+                    for b in range(2):
+                        h_codes, h_scales = hq[b, jq]
+                        nc.tensor.matmul_mx(
+                            out=bank[:, t, :],
+                            lhsT=wd_codes[:, b, 2 * t * P : 2 * (t + 1) * P].bitcast(FP4X4),
+                            lhsT_scale=wd_planes[:, b, t * P : (t + 1) * P],
+                            rhs=h_codes[:, cols].bitcast(FP8X4),
+                            rhs_scale=h_scales[:, cols],
+                            start=(b == 0),
+                            stop=(b == 1),
+                        )
+                g0 = (jq % 2) * JQ + half * P
+                nc.vector.tensor_tensor(result[:, :, cols], bank[:], gate[jq // 2][:, :, g0 : g0 + P], MULT)
+            nc.sync.dma_start(out=out_rows[:, :, jcols], in_=result[:])
+            pieces = TAIL if jq == NQ - 1 else [("scalar", 0, JQ)]
+            for engine, c0, c1 in pieces:
+                rounded = stage.tile([P, c1 - c0, PACK], BF16, name="out_rounded", align_bytes=64)
+                copy_on(
+                    engine,
+                    rounded[:].rearrange("p (c e) t -> p c t e", e=4),
+                    result[:, :, c0:c1].rearrange("p t (c e) -> p c t e", e=4),
+                )
+                nc.vector.quantize_mx(
+                    out=out_codes[:, jq * JQ + c0 : jq * JQ + c1].bitcast(FP8X4),
+                    scales=out_scales[:, jq * JQ + c0 : jq * JQ + c1],
+                    in_=rounded[:].rearrange("p j t -> p (j t)"),
+                )
+            if jq % 2 == 1:
+                jcols = slice((jq - 1) * JQ, (jq + 1) * JQ)
+                nc.sync.dma_start(out=out_words[:, jcols], in_=out_codes[:, jcols].bitcast(I32))
+
+        picked0 = gather_pass(0)
+        quantize_x(0, picked0, ["scalar"] * 4)
+        picked1 = gather_pass(1)
+        quantize_w("wg", 0, 0, "scalar")
+        quantize_w("wg", 1, 0, "vector")
+        quantize_x(1, picked1, ["scalar", "scalar", "scalar", "vector"])
+        quantize_w("wu", 0, 0, "vector")
+        quantize_w("wu", 1, 0, "vector")
+        gate_branch(0, 0)
+        gate_branch(0, 1)
+        up_branch(0, 0)
+        gate_branch(0, 2)
+        up_branch(0, 1)
+        gate_branch(0, 3)
+        quantize_w("wg", 0, 1, "scalar")
+        quantize_w("wg", 1, 1, "scalar")
+        quantize_w("wu", 0, 1, "scalar")
+        quantize_w("wu", 1, 1, "vector")
+        up_branch(0, 2)
+        up_branch(0, 3)
+        gate_branch(1, 0)
+        gate_branch(1, 1)
+        up_branch(1, 0)
+        gate_branch(1, 2)
+        up_branch(1, 1)
+        gate_branch(1, 3)
+        down(0)
+        up_branch(1, 2)
+        down(1)
+        up_branch(1, 3)
+        down(2)
+        down(3)
+        for q in range(4):
+            nc.scalar.dma_start(
+                out=out_2[0, 4 * q : 4 * q + 4, :].bitcast(I32),
+                in_=out_scales[32 * q : 32 * q + 4, :].bitcast(I32),
+            )

@@ -22,7 +22,10 @@ PASS = P * PACK
 JQ = 256
 NQ = J // JQ
 RAW_BUFS = 9
-TAIL = [("scalar", 0, 128), ("vector", 128, 256)]
+CUT7 = 4
+CUT0 = 1
+XBUFS = 4
+BANKS = (3, 3, 2)
 
 
 def tile_list_gelu_mulP_kernel(tc, xT, wgt, wg, wu, wd_words, wd_scales, g, offs, out_0, out_1, out_2):
@@ -35,7 +38,7 @@ def tile_list_gelu_mulP_kernel(tc, xT, wgt, wg, wu, wd_words, wd_scales, g, offs
         psum = ctx.enter_context(tc.psum_pool(name="psum", bufs=1))
 
         def copy_on(engine, out, in_):
-            if engine == "vector":
+            if engine == "v":
                 nc.vector.tensor_copy(out=out, in_=in_)
             else:
                 nc.scalar.copy(out=out, in_=in_)
@@ -85,7 +88,6 @@ def tile_list_gelu_mulP_kernel(tc, xT, wgt, wg, wu, wd_words, wd_scales, g, offs
         nc.vector.memset(wds_raw[:].bitcast(I32), 0)
         nc.sync.dma_start(offsets[:], offs)
         load_wd()
-        load_wds()
         load_place(0, 1024)
         load_x(0, 0)
         load_x(0, 1)
@@ -99,6 +101,7 @@ def tile_list_gelu_mulP_kernel(tc, xT, wgt, wg, wu, wd_words, wd_scales, g, offs
         load_w("wg", 1, 0)
         load_w("wu", 0, 0)
         load_w("wu", 1, 0)
+        load_wds()
         load_w("wg", 0, 1)
         load_w("wg", 1, 1)
         load_w("wu", 0, 1)
@@ -111,42 +114,56 @@ def tile_list_gelu_mulP_kernel(tc, xT, wgt, wg, wu, wd_words, wd_scales, g, offs
 
         wd_codes = keep.tile([P, 2, 2 * N], U8, name="wd_codes", align_bytes=64)
         wd_planes = keep.tile([P, 2, N], U8, name="wd_planes", align_bytes=64)
-        nc.vector.tensor_copy(
-            out=wd_codes[:].bitcast(U16).rearrange("p a (t m) -> p a m t", t=PACK),
-            in_=wd_raw[:].bitcast(U16).rearrange("p a (m t) -> p a m t", t=PACK),
-        )
-        nc.vector.tensor_copy(
-            out=wd_planes[:].rearrange("p a (t m) -> p a t m", t=PACK),
-            in_=wds_raw[:].rearrange("p a (m t) -> p a t m", t=PACK),
-        )
+
+        def deal_words():
+            nc.vector.tensor_copy(
+                out=wd_codes[:].bitcast(U16).rearrange("p a (t m) -> p a m t", t=PACK),
+                in_=wd_raw[:].bitcast(U16).rearrange("p a (m t) -> p a m t", t=PACK),
+            )
+
+        def deal_planes():
+            nc.vector.tensor_copy(
+                out=wd_planes[:].rearrange("p a (t m) -> p a t m", t=PACK),
+                in_=wds_raw[:].rearrange("p a (m t) -> p a t m", t=PACK),
+            )
 
         xq = {}
 
         def gather_pass(a):
             picked = stage.tile([P, PACK, J], F32, name="picked")
             for i in range(PACK):
-                nc.vector.tensor_tensor(picked[:, i, :], x_planes[a, i][:].indirect(offsets[:]), place_w[:], MULT)
+                cuts = {(0, 0): CUT0, (1, 3): CUT7}.get((a, i), 1)
+                for c in range(cuts):
+                    cols = slice(c * J // cuts, (c + 1) * J // cuts)
+                    part = offsets[:, c * 64 // cuts : (c + 1) * 64 // cuts]
+                    nc.vector.tensor_tensor(picked[:, i, cols], x_planes[a, i][:].indirect(part), place_w[:, cols], MULT)
             return picked
 
         def quantize_x(a, picked, engines):
-            for jq in range(NQ):
-                rounded = stage.tile([P, JQ, PACK], BF16, name="x_rounded", bufs=4, align_bytes=64)
+            width = J // len(engines)
+            for n, engine in enumerate(engines):
+                rounded = stage.tile([P, width, PACK], BF16, name="x_rounded", bufs=XBUFS, align_bytes=64)
                 copy_on(
-                    engines[jq],
+                    engine,
                     rounded[:].rearrange("p (c e) i -> p c i e", e=4),
-                    picked[:, :, jq * JQ : (jq + 1) * JQ].rearrange("p i (c e) -> p c i e", e=4),
+                    picked[:, :, n * width : (n + 1) * width].rearrange("p i (c e) -> p c i e", e=4),
                 )
-                xq[a, jq] = quantize(rounded[:].rearrange("p j i -> p (j i)"), JQ, "x%d%d" % (a, jq))
+                codes, scales = quantize(rounded[:].rearrange("p j i -> p (j i)"), width, "x%d%d" % (a, n))
+                for c0 in range(0, width, JQ):
+                    xq[a, (n * width + c0) // JQ] = codes[:, c0 : c0 + JQ], scales[:, c0 : c0 + JQ]
 
         wq = {}
 
-        def quantize_w(wname, a, b, engine):
+        def quantize_w(wname, a, b, engines):
             rounded = stage.tile([P, PACK * PASS], BF16, name="w_rounded", bufs=3, align_bytes=64)
-            copy_on(
-                engine,
-                rounded[:].rearrange("p (t m i) -> p m i t", t=PACK, i=PACK),
-                w_raw[wname, a, b][:].rearrange("p i (m t) -> p m i t", t=PACK),
-            )
+            share = P // len(engines)
+            for engine in sorted(set(engines)):
+                ms = slice(engines.index(engine) * share, (engines.index(engine) + engines.count(engine)) * share)
+                copy_on(
+                    engine,
+                    rounded[:].rearrange("p (t m i) -> p m i t", t=PACK, i=PACK)[:, ms, :, :],
+                    w_raw[wname, a, b][:].rearrange("p i (m t) -> p m i t", t=PACK)[:, ms, :, :],
+                )
             wq[wname, a, b] = quantize(rounded[:], PASS, "%s%d%d" % (wname, a, b))
 
         def first_product(out, wname, b, t, jq, cols):
@@ -168,7 +185,7 @@ def tile_list_gelu_mulP_kernel(tc, xT, wgt, wg, wu, wd_words, wd_scales, g, offs
         def gate_branch(b, jq):
             act[b, jq] = keep.tile([P, 2, JQ, 2], F32, name="act%d%d" % (b, jq))
             for tp in range(2):
-                bank = psum.tile([P, 2, JQ], F32, name="ga_bank", bufs=3)
+                bank = psum.tile([P, 2, JQ], F32, name="ga_bank", bufs=BANKS[0])
                 for e in range(2):
                     first_product(bank[:, e, :], "wg", b, 2 * tp + e, jq, slice(0, JQ))
                 nc.scalar.activation(out=act[b, jq][:, tp, :, :], in_=bank[:].rearrange("p e j -> p j e"), func=GELU)
@@ -179,7 +196,7 @@ def tile_list_gelu_mulP_kernel(tc, xT, wgt, wg, wu, wd_words, wd_scales, g, offs
             rounded = stage.tile([P, JQ, PACK], BF16, name="h_rounded", bufs=3, align_bytes=64)
             for half in range(2):
                 cols = slice(half * P, (half + 1) * P)
-                bank = psum.tile([P, PACK, P], F32, name="ub_bank", bufs=3)
+                bank = psum.tile([P, PACK, P], F32, name="ub_bank", bufs=BANKS[1])
                 for t in range(PACK):
                     first_product(bank[:, t, :], "wu", b, t, jq, cols)
                 nc.vector.tensor_tensor(
@@ -196,11 +213,14 @@ def tile_list_gelu_mulP_kernel(tc, xT, wgt, wg, wu, wd_words, wd_scales, g, offs
         out_words = out_1[0].rearrange("p j t -> p (j t)").bitcast(I32)
 
         def down(jq):
-            result = raw.tile([P, PACK, JQ], F32, name="result", tag="raw")
+            last = jq == NQ - 1
             jcols = slice(jq * JQ, (jq + 1) * JQ)
+            rounded = stage.tile([P, JQ, PACK], BF16, name="out_rounded", align_bytes=64)
+            if not last:
+                result = raw.tile([P, PACK, JQ], F32, name="result", tag="raw")
             for half in range(2):
                 cols = slice(half * P, (half + 1) * P)
-                bank = psum.tile([P, PACK, P], F32, name="y_bank", bufs=2)
+                bank = psum.tile([P, PACK, P], F32, name="y_bank", bufs=BANKS[2])
                 for t in range(PACK):
                     for b in range(2):
                         h_codes, h_scales = hq[b, jq]
@@ -214,51 +234,60 @@ def tile_list_gelu_mulP_kernel(tc, xT, wgt, wg, wu, wd_words, wd_scales, g, offs
                             stop=(b == 1),
                         )
                 g0 = (jq % 2) * JQ + half * P
-                nc.vector.tensor_tensor(result[:, :, cols], bank[:], gate[jq // 2][:, :, g0 : g0 + P], MULT)
-            nc.sync.dma_start(out=out_rows[:, :, jcols], in_=result[:])
-            pieces = TAIL if jq == NQ - 1 else [("scalar", 0, JQ)]
-            for engine, c0, c1 in pieces:
-                rounded = stage.tile([P, c1 - c0, PACK], BF16, name="out_rounded", align_bytes=64)
-                copy_on(
-                    engine,
-                    rounded[:].rearrange("p (c e) t -> p c t e", e=4),
-                    result[:, :, c0:c1].rearrange("p t (c e) -> p c t e", e=4),
+                if last:
+                    piece = raw.tile([P, PACK, P], F32, name="result", tag="raw")
+                    nc.vector.tensor_tensor(piece[:], bank[:], gate[jq // 2][:, :, g0 : g0 + P], MULT)
+                    nc.sync.dma_start(out=out_rows[:, :, jq * JQ + half * P : jq * JQ + (half + 1) * P], in_=piece[:])
+                    copy_on(
+                        "sv"[half],
+                        rounded[:, cols, :].rearrange("p (c e) t -> p c t e", e=4),
+                        piece[:].rearrange("p t (c e) -> p c t e", e=4),
+                    )
+                else:
+                    nc.vector.tensor_tensor(result[:, :, cols], bank[:], gate[jq // 2][:, :, g0 : g0 + P], MULT)
+            if not last:
+                nc.sync.dma_start(out=out_rows[:, :, jcols], in_=result[:])
+                nc.scalar.copy(
+                    out=rounded[:].rearrange("p (c e) t -> p c t e", e=4),
+                    in_=result[:].rearrange("p t (c e) -> p c t e", e=4),
                 )
-                nc.vector.quantize_mx(
-                    out=out_codes[:, jq * JQ + c0 : jq * JQ + c1].bitcast(FP8X4),
-                    scales=out_scales[:, jq * JQ + c0 : jq * JQ + c1],
-                    in_=rounded[:].rearrange("p j t -> p (j t)"),
-                )
+            nc.vector.quantize_mx(
+                out=out_codes[:, jcols].bitcast(FP8X4),
+                scales=out_scales[:, jcols],
+                in_=rounded[:].rearrange("p j t -> p (j t)"),
+            )
             if jq % 2 == 1:
-                jcols = slice((jq - 1) * JQ, (jq + 1) * JQ)
-                nc.sync.dma_start(out=out_words[:, jcols], in_=out_codes[:, jcols].bitcast(I32))
+                pair = slice((jq - 1) * JQ, (jq + 1) * JQ)
+                nc.sync.dma_start(out=out_words[:, pair], in_=out_codes[:, pair].bitcast(I32))
 
         picked0 = gather_pass(0)
-        quantize_x(0, picked0, ["scalar"] * 4)
+        quantize_x(0, picked0, "ssss")
         picked1 = gather_pass(1)
-        quantize_w("wg", 0, 0, "scalar")
-        quantize_w("wg", 1, 0, "vector")
-        quantize_x(1, picked1, ["scalar", "scalar", "scalar", "vector"])
-        quantize_w("wu", 0, 0, "vector")
-        quantize_w("wu", 1, 0, "vector")
+        quantize_w("wg", 1, 0, "v")
+        quantize_w("wg", 0, 0, "s")
+        quantize_x(1, picked1, "ssss")
+        quantize_w("wu", 0, 0, "vs")
+        quantize_w("wu", 1, 0, "v")
         gate_branch(0, 0)
         gate_branch(0, 1)
-        up_branch(0, 0)
         gate_branch(0, 2)
-        up_branch(0, 1)
         gate_branch(0, 3)
-        quantize_w("wg", 0, 1, "scalar")
-        quantize_w("wg", 1, 1, "scalar")
-        quantize_w("wu", 0, 1, "scalar")
-        quantize_w("wu", 1, 1, "vector")
+        quantize_w("wg", 0, 1, "v")
+        quantize_w("wg", 1, 1, "s")
+        quantize_w("wu", 0, 1, "s")
+        quantize_w("wu", 1, 1, "v")
+        up_branch(0, 0)
+        up_branch(0, 1)
         up_branch(0, 2)
         up_branch(0, 3)
         gate_branch(1, 0)
         gate_branch(1, 1)
-        up_branch(1, 0)
         gate_branch(1, 2)
-        up_branch(1, 1)
         gate_branch(1, 3)
+        deal_words()
+        deal_planes()
+        up_branch(1, 0)
+        up_branch(1, 1)
         down(0)
         up_branch(1, 2)
         down(1)

@@ -22,7 +22,9 @@ PASS = P * PACK
 JQ = 256
 NQ = J // JQ
 RAW_BUFS = 9
-CUT7 = 4
+WBUFS = 2
+PAIRS = 1
+CUT7 = 2
 CUT0 = 1
 XBUFS = 4
 BANKS = (3, 3, 2)
@@ -51,7 +53,7 @@ def tile_list_gelu_mulP_kernel(tc, xT, wgt, wg, wu, wd_words, wd_scales, g, offs
 
         offsets = keep.tile([P, J // 16], U16, name="offsets")
         wd_raw = keep.tile([P, 2, 2 * N], U8, name="wd_raw")
-        wds_raw = keep.tile([P, 2, N], U8, name="wds_raw")
+        wds_raw = keep.tile([P, N], U8, name="wds_raw")
         place_w = keep.tile([P, J], F32, name="place_w")
         x_planes = {}
         w_raw = {}
@@ -63,8 +65,8 @@ def tile_list_gelu_mulP_kernel(tc, xT, wgt, wg, wu, wd_words, wd_scales, g, offs
         def load_wds():
             for q in range(4):
                 nc.sync.dma_start(
-                    out=wds_raw[32 * q : 32 * q + 4, :, :].bitcast(I32),
-                    in_=wd_scales[:, 4 * q : 4 * q + 4, :].rearrange("a r n -> r a n").bitcast(I32),
+                    out=wds_raw[32 * q : 32 * q + 8, :].bitcast(I32),
+                    in_=wd_scales[:, 4 * q : 4 * q + 4, :].bitcast(I32),
                 )
 
         def load_place(c0, c1):
@@ -113,7 +115,8 @@ def tile_list_gelu_mulP_kernel(tc, xT, wgt, wg, wu, wd_words, wd_scales, g, offs
         nc.scalar.activation(out=warm[:], in_=place_w[:, 0:1], func=GELU)
 
         wd_codes = keep.tile([P, 2, 2 * N], U8, name="wd_codes", align_bytes=64)
-        wd_planes = keep.tile([P, 2, N], U8, name="wd_planes", align_bytes=64)
+        wd_planes = [keep.tile([P, N], U8, name="wd_plane%d" % b, align_bytes=64) for b in range(2)]
+        nc.vector.memset(wd_planes[1][:].bitcast(I32), 0)
 
         def deal_words():
             nc.vector.tensor_copy(
@@ -123,14 +126,20 @@ def tile_list_gelu_mulP_kernel(tc, xT, wgt, wg, wu, wd_words, wd_scales, g, offs
 
         def deal_planes():
             nc.vector.tensor_copy(
-                out=wd_planes[:].rearrange("p a (t m) -> p a t m", t=PACK),
-                in_=wds_raw[:].rearrange("p a (m t) -> p a t m", t=PACK),
+                out=wd_planes[0][:].rearrange("p (t m) -> p t m", t=PACK),
+                in_=wds_raw[:].rearrange("p (m t) -> p t m", t=PACK),
             )
+            for q in range(4):
+                nc.sync.dma_start(
+                    out=wd_planes[1][32 * q : 32 * q + 4, :].bitcast(I32),
+                    in_=wd_planes[0][32 * q + 4 : 32 * q + 8, :].bitcast(I32),
+                )
 
         xq = {}
 
         def gather_pass(a):
-            picked = stage.tile([P, PACK, J], F32, name="picked")
+            picked_flat = stage.tile([P, PACK * J], F32, name="picked")
+            picked = picked_flat[:].rearrange("p (i j) -> p i j", i=PACK)
             for i in range(PACK):
                 cuts = {(0, 0): CUT0, (1, 3): CUT7}.get((a, i), 1)
                 for c in range(cuts):
@@ -141,39 +150,45 @@ def tile_list_gelu_mulP_kernel(tc, xT, wgt, wg, wu, wd_words, wd_scales, g, offs
 
         def quantize_x(a, picked, engines):
             width = J // len(engines)
-            for n, engine in enumerate(engines):
-                rounded = stage.tile([P, width, PACK], BF16, name="x_rounded", bufs=XBUFS, align_bytes=64)
-                copy_on(
-                    engine,
-                    rounded[:].rearrange("p (c e) i -> p c i e", e=4),
-                    picked[:, :, n * width : (n + 1) * width].rearrange("p i (c e) -> p c i e", e=4),
-                )
-                codes, scales = quantize(rounded[:].rearrange("p j i -> p (j i)"), width, "x%d%d" % (a, n))
-                for c0 in range(0, width, JQ):
-                    xq[a, (n * width + c0) // JQ] = codes[:, c0 : c0 + JQ], scales[:, c0 : c0 + JQ]
+            steps = PAIRS if a == 1 else 1
+            share = PACK // steps
+            tiles = [stage.tile([P, width, PACK], BF16, name="x_rounded", bufs=XBUFS, align_bytes=64) for engine in engines]
+            for step in range(steps):
+                planes = slice(step * share, (step + 1) * share)
+                for n, engine in enumerate(engines):
+                    copy_on(
+                        engine,
+                        tiles[n][:, :, planes].rearrange("p (c e) i -> p c i e", e=4),
+                        picked[:, planes, n * width : (n + 1) * width].rearrange("p i (c e) -> p c i e", e=4),
+                    )
+                    if step == steps - 1:
+                        codes, scales = quantize(tiles[n][:].rearrange("p j i -> p (j i)"), width, "x%d%d" % (a, n))
+                        for c0 in range(0, width, JQ):
+                            xq[a, (n * width + c0) // JQ] = codes[:, c0 : c0 + JQ], scales[:, c0 : c0 + JQ]
 
         wq = {}
 
         def quantize_w(wname, a, b, engines):
-            rounded = stage.tile([P, PACK * PASS], BF16, name="w_rounded", bufs=3, align_bytes=64)
-            share = P // len(engines)
-            for engine in sorted(set(engines)):
-                ms = slice(engines.index(engine) * share, (engines.index(engine) + engines.count(engine)) * share)
+            share = PACK // len(engines)
+            for n, engine in enumerate(engines):
+                rounded = stage.tile([P, share * PASS], BF16, name="w_rounded", tag="rounded_" + engine, bufs={"v": 4, "s": 2}[engine], align_bytes=64)
                 copy_on(
                     engine,
-                    rounded[:].rearrange("p (t m i) -> p m i t", t=PACK, i=PACK)[:, ms, :, :],
-                    w_raw[wname, a, b][:].rearrange("p i (m t) -> p m i t", t=PACK)[:, ms, :, :],
+                    rounded[:].rearrange("p (t m i) -> p m i t", t=share, i=PACK),
+                    w_raw[wname, a, b][:].rearrange("p i (m t) -> p m i t", t=PACK)[:, :, :, n * share : (n + 1) * share],
                 )
-            wq[wname, a, b] = quantize(rounded[:], PASS, "%s%d%d" % (wname, a, b))
+                codes, scales = quantize(rounded[:], share * P, "%s%d%d%d" % (wname, a, b, n))
+                for e in range(share):
+                    wq[wname, a, b, n * share + e] = codes[:, e * P : (e + 1) * P], scales[:, e * P : (e + 1) * P]
 
         def first_product(out, wname, b, t, jq, cols):
             for a in range(2):
-                w_codes, w_scales = wq[wname, a, b]
+                w_codes, w_scales = wq[wname, a, b, t]
                 x_codes, x_scales = xq[a, jq]
                 nc.tensor.matmul_mx(
                     out=out,
-                    lhsT=w_codes[:, t * P : (t + 1) * P].bitcast(FP8X4),
-                    lhsT_scale=w_scales[:, t * P : (t + 1) * P],
+                    lhsT=w_codes.bitcast(FP8X4),
+                    lhsT_scale=w_scales,
                     rhs=x_codes[:, cols].bitcast(FP8X4),
                     rhs_scale=x_scales[:, cols],
                     start=(a == 0),
@@ -193,7 +208,7 @@ def tile_list_gelu_mulP_kernel(tc, xT, wgt, wg, wu, wd_words, wd_scales, g, offs
         hq = {}
 
         def up_branch(b, jq):
-            rounded = stage.tile([P, JQ, PACK], BF16, name="h_rounded", bufs=3, align_bytes=64)
+            rounded = stage.tile([P, JQ, PACK], BF16, name="h_rounded", tag="rounded_v", bufs=4, align_bytes=64)
             for half in range(2):
                 cols = slice(half * P, (half + 1) * P)
                 bank = psum.tile([P, PACK, P], F32, name="ub_bank", bufs=BANKS[1])
@@ -212,10 +227,23 @@ def tile_list_gelu_mulP_kernel(tc, xT, wgt, wg, wu, wd_words, wd_scales, g, offs
         out_rows = out_0.rearrange("(p t) j -> p t j", t=PACK)
         out_words = out_1[0].rearrange("p j t -> p (j t)").bitcast(I32)
 
+        def hand_on(result, c0, width, engine):
+            cols = slice(c0, c0 + width)
+            nc.sync.dma_start(out=out_rows[:, :, cols], in_=result[:])
+            rounded = stage.tile([P, width, PACK], BF16, name="out_rounded", align_bytes=64)
+            copy_on(
+                engine,
+                rounded[:].rearrange("p (c e) t -> p c t e", e=4),
+                result[:].rearrange("p t (c e) -> p c t e", e=4),
+            )
+            nc.vector.quantize_mx(
+                out=out_codes[:, cols].bitcast(FP8X4),
+                scales=out_scales[:, cols],
+                in_=rounded[:].rearrange("p j t -> p (j t)"),
+            )
+
         def down(jq):
             last = jq == NQ - 1
-            jcols = slice(jq * JQ, (jq + 1) * JQ)
-            rounded = stage.tile([P, JQ, PACK], BF16, name="out_rounded", align_bytes=64)
             if not last:
                 result = raw.tile([P, PACK, JQ], F32, name="result", tag="raw")
             for half in range(2):
@@ -227,7 +255,7 @@ def tile_list_gelu_mulP_kernel(tc, xT, wgt, wg, wu, wd_words, wd_scales, g, offs
                         nc.tensor.matmul_mx(
                             out=bank[:, t, :],
                             lhsT=wd_codes[:, b, 2 * t * P : 2 * (t + 1) * P].bitcast(FP4X4),
-                            lhsT_scale=wd_planes[:, b, t * P : (t + 1) * P],
+                            lhsT_scale=wd_planes[b][:, t * P : (t + 1) * P],
                             rhs=h_codes[:, cols].bitcast(FP8X4),
                             rhs_scale=h_scales[:, cols],
                             start=(b == 0),
@@ -237,58 +265,44 @@ def tile_list_gelu_mulP_kernel(tc, xT, wgt, wg, wu, wd_words, wd_scales, g, offs
                 if last:
                     piece = raw.tile([P, PACK, P], F32, name="result", tag="raw")
                     nc.vector.tensor_tensor(piece[:], bank[:], gate[jq // 2][:, :, g0 : g0 + P], MULT)
-                    nc.sync.dma_start(out=out_rows[:, :, jq * JQ + half * P : jq * JQ + (half + 1) * P], in_=piece[:])
-                    copy_on(
-                        "sv"[half],
-                        rounded[:, cols, :].rearrange("p (c e) t -> p c t e", e=4),
-                        piece[:].rearrange("p t (c e) -> p c t e", e=4),
-                    )
+                    hand_on(piece, jq * JQ + half * P, P, "sv"[half])
                 else:
                     nc.vector.tensor_tensor(result[:, :, cols], bank[:], gate[jq // 2][:, :, g0 : g0 + P], MULT)
             if not last:
-                nc.sync.dma_start(out=out_rows[:, :, jcols], in_=result[:])
-                nc.scalar.copy(
-                    out=rounded[:].rearrange("p (c e) t -> p c t e", e=4),
-                    in_=result[:].rearrange("p t (c e) -> p c t e", e=4),
-                )
-            nc.vector.quantize_mx(
-                out=out_codes[:, jcols].bitcast(FP8X4),
-                scales=out_scales[:, jcols],
-                in_=rounded[:].rearrange("p j t -> p (j t)"),
-            )
+                hand_on(result, jq * JQ, JQ, "s")
             if jq % 2 == 1:
                 pair = slice((jq - 1) * JQ, (jq + 1) * JQ)
                 nc.sync.dma_start(out=out_words[:, pair], in_=out_codes[:, pair].bitcast(I32))
 
         picked0 = gather_pass(0)
-        quantize_x(0, picked0, "ssss")
+        quantize_x(0, picked0, "ss")
         picked1 = gather_pass(1)
-        quantize_w("wg", 1, 0, "v")
+        deal_words()
         quantize_w("wg", 0, 0, "s")
-        quantize_x(1, picked1, "ssss")
-        quantize_w("wu", 0, 0, "vs")
+        quantize_w("wg", 1, 0, "v")
+        quantize_x(1, picked1, "ss")
+        quantize_w("wu", 0, 0, "v")
         quantize_w("wu", 1, 0, "v")
+        quantize_w("wg", 0, 1, "vs")
+        quantize_w("wg", 1, 1, "s")
+        deal_planes()
         gate_branch(0, 0)
         gate_branch(0, 1)
-        gate_branch(0, 2)
-        gate_branch(0, 3)
-        quantize_w("wg", 0, 1, "v")
-        quantize_w("wg", 1, 1, "s")
-        quantize_w("wu", 0, 1, "s")
-        quantize_w("wu", 1, 1, "v")
         up_branch(0, 0)
+        gate_branch(0, 2)
         up_branch(0, 1)
-        up_branch(0, 2)
-        up_branch(0, 3)
+        gate_branch(0, 3)
+        quantize_w("wu", 0, 1, "s")
         gate_branch(1, 0)
         gate_branch(1, 1)
-        gate_branch(1, 2)
-        gate_branch(1, 3)
-        deal_words()
-        deal_planes()
+        up_branch(0, 2)
+        quantize_w("wu", 1, 1, "v")
+        up_branch(0, 3)
         up_branch(1, 0)
+        gate_branch(1, 2)
         up_branch(1, 1)
         down(0)
+        gate_branch(1, 3)
         up_branch(1, 2)
         down(1)
         up_branch(1, 3)

from contextlib import ExitStack

import concourse.mybir as mybir

K, R, N, T, J = 1024, 1024, 512, 2048, 1024
FLOPS = 2 * K * R * J * 2 + 2 * R * N * J

F32 = mybir.dt.float32
BF16 = mybir.dt.bfloat16
I32 = mybir.dt.int32
U32 = mybir.dt.uint32
U16 = mybir.dt.uint16
U8 = mybir.dt.uint8
FP8X4 = mybir.dt.float8_e4m3fn_x4
FP4X4 = mybir.dt.float4_e2m1fn_x4
MULT = mybir.AluOpType.mult
GELU = mybir.ActivationFunctionType.Gelu_apprx_tanh

P = 128
PACK = 4
PASS = P * PACK
JQ = 256
NQ = J // JQ
RAW_BUFS = 9
WBUFS = 2
PAIRS = 1
CUT7 = 2
CUT0 = 1
XBUFS = 4
BANKS = (3, 3, 2)


def tile_list_gelu_mulP_kernel(tc, xT, wgt, wg, wu, wd_words, wd_scales, g, offs, out_0, out_1, out_2):
    nc = tc.nc

    with ExitStack() as ctx:
        keep = ctx.enter_context(tc.tile_pool(name="keep", bufs=1))
        raw = ctx.enter_context(tc.tile_pool(name="raw", bufs=RAW_BUFS))
        stage = ctx.enter_context(tc.tile_pool(name="stage", bufs=2))
        psum = ctx.enter_context(tc.psum_pool(name="psum", bufs=1))

        def copy_on(engine, out, in_):
            if engine == "v":
                nc.vector.tensor_copy(out=out, in_=in_)
            else:
                nc.scalar.copy(out=out, in_=in_)

        def quantize(rounded, width, name):
            codes = keep.tile([P, width], U32, name=name + "_codes", align_bytes=64)
            scales = keep.tile([P, width], U8, name=name + "_scales", align_bytes=64)
            nc.vector.quantize_mx(out=codes[:].bitcast(FP8X4), scales=scales[:], in_=rounded)
            return codes, scales

        offsets = keep.tile([P, J // 16], U16, name="offsets")
        wd_raw = keep.tile([P, 2, 2 * N], U8, name="wd_raw")
        wds_raw = keep.tile([P, N], U8, name="wds_raw")
        place_w = keep.tile([P, J], F32, name="place_w")
        x_planes = {}
        w_raw = {}
        gate = {}

        def load_wd():
            nc.sync.dma_start(out=wd_raw[:].bitcast(I32), in_=wd_words.rearrange("a p n -> p a n").bitcast(I32))

        def load_wds():
            for q in range(4):
                nc.sync.dma_start(
                    out=wds_raw[32 * q : 32 * q + 8, :].bitcast(I32),
                    in_=wd_scales[:, 4 * q : 4 * q + 4, :].bitcast(I32),
                )

        def load_place(c0, c1):
            nc.sync.dma_start(out=place_w[:, c0:c1], in_=wgt[:, c0:c1])

        def load_x(a, i):
            rows = xT[a * PASS : (a + 1) * PASS, :].rearrange("(p i) t -> p i t", i=PACK)
            x_planes[a, i] = raw.tile([P, T], F32, name="x_plane", tag="raw")
            nc.sync.dma_start(out=x_planes[a, i][:], in_=rows[:, i, :])

        def load_w(wname, a, b):
            w = {"wg": wg, "wu": wu}[wname]
            w_raw[wname, a, b] = raw.tile([P, PACK, PASS], F32, name="w_raw", tag="raw")
            block = w[a * PASS : (a + 1) * PASS, b * PASS : (b + 1) * PASS]
            nc.sync.dma_start(out=w_raw[wname, a, b][:], in_=block.rearrange("(p i) c -> p i c", i=PACK))

        def load_g(h):
            gate[h] = raw.tile([P, PACK, 512], F32, name="gate", tag="raw")
            nc.sync.dma_start(out=gate[h][:], in_=g[:, h * 512 : (h + 1) * 512].rearrange("(p t) j -> p t j", t=PACK))

        nc.vector.memset(wds_raw[:].bitcast(I32), 0)
        nc.sync.dma_start(offsets[:], offs)
        load_wd()
        load_place(0, 1024)
        load_x(0, 0)
        load_x(0, 1)
        load_x(0, 2)
        load_x(0, 3)
        load_x(1, 0)
        load_x(1, 1)
        load_x(1, 2)
        load_w("wg", 0, 0)
        load_x(1, 3)
        load_w("wg", 1, 0)
        load_w("wu", 0, 0)
        load_w("wu", 1, 0)
        load_wds()
        load_w("wg", 0, 1)
        load_w("wg", 1, 1)
        load_w("wu", 0, 1)
        load_w("wu", 1, 1)
        load_g(0)
        load_g(1)

        warm = keep.tile([P, 1], F32, name="warm")
        nc.scalar.activation(out=warm[:], in_=place_w[:, 0:1], func=GELU)

        wd_codes = keep.tile([P, 2, 2 * N], U8, name="wd_codes", align_bytes=64)
        wd_planes = [keep.tile([P, N], U8, name="wd_plane%d" % b, align_bytes=64) for b in range(2)]
        nc.vector.memset(wd_planes[1][:].bitcast(I32), 0)

        def deal_words():
            nc.vector.tensor_copy(
                out=wd_codes[:].bitcast(U16).rearrange("p a (t m) -> p a m t", t=PACK),
                in_=wd_raw[:].bitcast(U16).rearrange("p a (m t) -> p a m t", t=PACK),
            )

        def deal_planes():
            nc.vector.tensor_copy(
                out=wd_planes[0][:].rearrange("p (t m) -> p t m", t=PACK),
                in_=wds_raw[:].rearrange("p (m t) -> p t m", t=PACK),
            )
            for q in range(4):
                nc.sync.dma_start(
                    out=wd_planes[1][32 * q : 32 * q + 4, :].bitcast(I32),
                    in_=wd_planes[0][32 * q + 4 : 32 * q + 8, :].bitcast(I32),
                )

        xq = {}

        def gather_pass(a):
            picked_flat = stage.tile([P, PACK * J], F32, name="picked")
            picked = picked_flat[:].rearrange("p (i j) -> p i j", i=PACK)
            for i in range(PACK):
                cuts = {(0, 0): CUT0, (1, 3): CUT7}.get((a, i), 1)
                for c in range(cuts):
                    cols = slice(c * J // cuts, (c + 1) * J // cuts)
                    part = offsets[:, c * 64 // cuts : (c + 1) * 64 // cuts]
                    nc.vector.tensor_tensor(picked[:, i, cols], x_planes[a, i][:].indirect(part), place_w[:, cols], MULT)
            return picked

        def quantize_x(a, picked, engines):
            width = J // len(engines)
            steps = PAIRS if a == 1 else 1
            share = PACK // steps
            tiles = [stage.tile([P, width, PACK], BF16, name="x_rounded", bufs=XBUFS, align_bytes=64) for engine in engines]
            for step in range(steps):
                planes = slice(step * share, (step + 1) * share)
                for n, engine in enumerate(engines):
                    copy_on(
                        engine,
                        tiles[n][:, :, planes].rearrange("p (c e) i -> p c i e", e=4),
                        picked[:, planes, n * width : (n + 1) * width].rearrange("p i (c e) -> p c i e", e=4),
                    )
                    if step == steps - 1:
                        codes, scales = quantize(tiles[n][:].rearrange("p j i -> p (j i)"), width, "x%d%d" % (a, n))
                        for c0 in range(0, width, JQ):
                            xq[a, (n * width + c0) // JQ] = codes[:, c0 : c0 + JQ], scales[:, c0 : c0 + JQ]

        wq = {}

        def quantize_w(wname, a, b, engines):
            share = PACK // len(engines)
            for n, engine in enumerate(engines):
                rounded = stage.tile([P, share * PASS], BF16, name="w_rounded", tag="rounded_" + engine, bufs={"v": 4, "s": 2}[engine], align_bytes=64)
                copy_on(
                    engine,
                    rounded[:].rearrange("p (t m i) -> p m i t", t=share, i=PACK),
                    w_raw[wname, a, b][:].rearrange("p i (m t) -> p m i t", t=PACK)[:, :, :, n * share : (n + 1) * share],
                )
                codes, scales = quantize(rounded[:], share * P, "%s%d%d%d" % (wname, a, b, n))
                for e in range(share):
                    wq[wname, a, b, n * share + e] = codes[:, e * P : (e + 1) * P], scales[:, e * P : (e + 1) * P]

        def first_product(out, wname, b, t, jq, cols):
            for a in range(2):
                w_codes, w_scales = wq[wname, a, b, t]
                x_codes, x_scales = xq[a, jq]
                nc.tensor.matmul_mx(
                    out=out,
                    lhsT=w_codes.bitcast(FP8X4),
                    lhsT_scale=w_scales,
                    rhs=x_codes[:, cols].bitcast(FP8X4),
                    rhs_scale=x_scales[:, cols],
                    start=(a == 0),
                    stop=(a == 1),
                )

        act = {}

        def gate_branch(b, jq):
            act[b, jq] = keep.tile([P, 2, JQ, 2], F32, name="act%d%d" % (b, jq))
            for tp in range(2):
                bank = psum.tile([P, 2, JQ], F32, name="ga_bank", bufs=BANKS[0])
                for e in range(2):
                    first_product(bank[:, e, :], "wg", b, 2 * tp + e, jq, slice(0, JQ))
                nc.scalar.activation(out=act[b, jq][:, tp, :, :], in_=bank[:].rearrange("p e j -> p j e"), func=GELU)

        hq = {}

        def up_branch(b, jq):
            rounded = stage.tile([P, JQ, PACK], BF16, name="h_rounded", tag="rounded_v", bufs=4, align_bytes=64)
            for half in range(2):
                cols = slice(half * P, (half + 1) * P)
                bank = psum.tile([P, PACK, P], F32, name="ub_bank", bufs=BANKS[1])
                for t in range(PACK):
                    first_product(bank[:, t, :], "wu", b, t, jq, cols)
                nc.vector.tensor_tensor(
                    rounded[:, cols, :].rearrange("p j (tp e) -> p j tp e", e=2),
                    bank[:].rearrange("p (tp e) j -> p j tp e", e=2),
                    act[b, jq][:, :, cols, :].rearrange("p tp j e -> p j tp e"),
                    MULT,
                )
            hq[b, jq] = quantize(rounded[:].rearrange("p j t -> p (j t)"), JQ, "h%d%d" % (b, jq))

        out_codes = keep.tile([P, J], U32, name="out_codes", align_bytes=64)
        out_scales = keep.tile([P, J], U8, name="out_scales", align_bytes=64)
        out_rows = out_0.rearrange("(p t) j -> p t j", t=PACK)
        out_words = out_1[0].rearrange("p j t -> p (j t)").bitcast(I32)

        def hand_on(result, c0, width, engine):
            cols = slice(c0, c0 + width)
            nc.sync.dma_start(out=out_rows[:, :, cols], in_=result[:])
            rounded = stage.tile([P, width, PACK], BF16, name="out_rounded", align_bytes=64)
            copy_on(
                engine,
                rounded[:].rearrange("p (c e) t -> p c t e", e=4),
                result[:].rearrange("p t (c e) -> p c t e", e=4),
            )
            nc.vector.quantize_mx(
                out=out_codes[:, cols].bitcast(FP8X4),
                scales=out_scales[:, cols],
                in_=rounded[:].rearrange("p j t -> p (j t)"),
            )

        def down(jq):
            last = jq == NQ - 1
            if not last:
                result = raw.tile([P, PACK, JQ], F32, name="result", tag="raw")
            for half in range(2):
                cols = slice(half * P, (half + 1) * P)
                bank = psum.tile([P, PACK, P], F32, name="y_bank", bufs=BANKS[2])
                for t in range(PACK):
                    for b in range(2):
                        h_codes, h_scales = hq[b, jq]
                        nc.tensor.matmul_mx(
                            out=bank[:, t, :],
                            lhsT=wd_codes[:, b, 2 * t * P : 2 * (t + 1) * P].bitcast(FP4X4),
                            lhsT_scale=wd_planes[b][:, t * P : (t + 1) * P],
                            rhs=h_codes[:, cols].bitcast(FP8X4),
                            rhs_scale=h_scales[:, cols],
                            start=(b == 0),
                            stop=(b == 1),
                        )
                g0 = (jq % 2) * JQ + half * P
                if last:
                    piece = raw.tile([P, PACK, P], F32, name="result", tag="raw")
                    nc.vector.tensor_tensor(piece[:], bank[:], gate[jq // 2][:, :, g0 : g0 + P], MULT)
                    hand_on(piece, jq * JQ + half * P, P, "sv"[half])
                else:
                    nc.vector.tensor_tensor(result[:, :, cols], bank[:], gate[jq // 2][:, :, g0 : g0 + P], MULT)
            if not last:
                hand_on(result, jq * JQ, JQ, "s")
            if jq % 2 == 1:
                pair = slice((jq - 1) * JQ, (jq + 1) * JQ)
                nc.sync.dma_start(out=out_words[:, pair], in_=out_codes[:, pair].bitcast(I32))

        picked0 = gather_pass(0)
        quantize_x(0, picked0, "ss")
        picked1 = gather_pass(1)
        deal_words()
        quantize_w("wg", 0, 0, "s")
        quantize_w("wg", 1, 0, "v")
        quantize_x(1, picked1, "ss")
        quantize_w("wu", 0, 0, "v")
        quantize_w("wu", 1, 0, "v")
        quantize_w("wg", 0, 1, "vs")
        quantize_w("wg", 1, 1, "s")
        deal_planes()
        gate_branch(0, 0)
        gate_branch(0, 1)
        up_branch(0, 0)
        gate_branch(0, 2)
        up_branch(0, 1)
        gate_branch(0, 3)
        quantize_w("wu", 0, 1, "s")
        gate_branch(1, 0)
        gate_branch(1, 1)
        up_branch(0, 2)
        quantize_w("wu", 1, 1, "v")
        up_branch(0, 3)
        up_branch(1, 0)
        gate_branch(1, 2)
        up_branch(1, 1)
        down(0)
        gate_branch(1, 3)
        up_branch(1, 2)
        down(1)
        up_branch(1, 3)
        down(2)
        down(3)
        for q in range(4):
            nc.scalar.dma_start(
                out=out_2[0, 4 * q : 4 * q + 4, :].bitcast(I32),
                in_=out_scales[32 * q : 32 * q + 4, :].bitcast(I32),
            )
